import numpy as np
import ml_dtypes


def mxq(x, axis, fmt="e4m3"):
    dtype, down = {"e4m3": (ml_dtypes.float8_e4m3fn, 7), "e5m2": (ml_dtypes.float8_e5m2, 14)}[fmt]
    v = np.moveaxis(np.asarray(x, np.float32).astype(ml_dtypes.bfloat16).astype(np.float64), axis, -1)
    blocks = v.reshape(v.shape[:-1] + (-1, 32))
    amax = np.abs(blocks).max(-1, keepdims=True)
    byte = np.maximum(np.where(amax > 0, np.frexp(amax)[1] - 1 + 127, 0) - down, 1)
    scale = np.exp2(byte - 127.0)
    codes = (blocks / scale).astype(np.float32).astype(dtype).astype(np.float64)
    return np.moveaxis((codes * scale).reshape(v.shape), -1, axis)


WIDE = False


def mx_kscale(k):
    if not WIDE:
        return np.ones(k)
    levels = np.array([10, -10, 5, -5, 0])
    if k % 512:
        return np.exp2(np.random.permutation(np.resize(levels, k // 32))).repeat(32)
    a = np.empty((k // 512, 16))
    for p in range(k // 512):
        a[p, :8] = np.random.permutation(np.resize(levels, 8))
        for g in range(8):
            far = levels[np.abs(levels - a[p, g]) >= 10]
            a[p, g + 8] = far[np.random.randint(len(far))]
    return np.exp2(a.ravel()).repeat(32)


BF16 = ml_dtypes.bfloat16


def bf(x):
    return np.asarray(x, np.float32).astype(BF16)


def f64(x):
    return np.asarray(x).astype(np.float64)


E2M1 = np.array([0.0, 0.5, 1.0, 1.5, 2.0, 3.0, 4.0, 6.0, -0.0, -0.5, -1.0, -1.5, -2.0, -3.0, -4.0, -6.0])


def pack_weight(w, fmt):
    k, n = w.shape
    w = f64(bf(w)).reshape(k // 32, 32, n)
    amax = np.abs(w).max(1)
    if fmt == "e4m3":
        byte = np.frexp(amax)[1] - 1 + 127 - 7
    else:
        mant, ex = np.frexp(amax / 6.0)
        byte = np.where(mant > 0.5, ex, ex - 1) + 127
    byte = np.clip(np.where(amax > 0, byte, 1), 1, 254)
    scaled = (w * np.exp2(127.0 - byte)[:, None, :]).reshape(k, n).astype(np.float32)
    by_word = np.ascontiguousarray(scaled.reshape(k // 512, 128, 4, n).transpose(0, 1, 3, 2))
    if fmt == "e4m3":
        words = by_word.astype(ml_dtypes.float8_e4m3fn).view(np.uint8)
    else:
        c = by_word.astype(ml_dtypes.float4_e2m1fn).view(np.uint8) & 0xF
        words = c[..., 0::2] | (c[..., 1::2] << 4)
    return np.ascontiguousarray(words), np.ascontiguousarray(byte.astype(np.uint8).reshape(k // 512, 16, n))


def unpack_weight(words, scales, fmt):
    g, p, n, _ = words.shape
    if fmt == "e4m3":
        vals = np.ascontiguousarray(words).view(ml_dtypes.float8_e4m3fn).astype(np.float64)
    else:
        nib = np.empty((g, p, n, 4), np.uint8)
        nib[..., 0::2] = words & 0xF
        nib[..., 1::2] = words >> 4
        vals = E2M1[nib]
    vals = vals * np.repeat(np.exp2(scales.astype(np.float64) - 127.0), 8, axis=1)[..., None]
    return vals.transpose(0, 1, 3, 2).reshape(g * 512, n)
def pack4(w):
    words, scales = pack_weight(w, "e2m1")
    return words.reshape(words.shape[0], 128, -1), scales


def unpack4(words, scales):
    return unpack_weight(words.reshape(words.shape[0], 128, -1, 2), scales, "e2m1")


def planes(Y):
    n, m = Y.shape
    b = f64(bf(Y)).reshape(n // 32, 32, m)
    amax = np.abs(b).max(1)
    byte = np.clip(np.where(amax > 0, np.frexp(amax)[1] - 1 + 127 - 7, 1), 1, 254)
    codes = (b * np.exp2(127.0 - byte)[:, None, :]).reshape(n, m).astype(np.float32).astype(ml_dtypes.float8_e4m3fn).view(np.uint8)
    words = codes.reshape(n // 512, 128, 4, m).transpose(0, 1, 3, 2)
    return np.ascontiguousarray(words), np.ascontiguousarray(byte.astype(np.uint8).reshape(n // 512, 16, m))


F, P, KW, KS = 512, 2048, 1536, 512

def field_rows(k):
    re, im = np.random.randn(F, k // 2), np.random.randn(F, k // 2)
    return np.concatenate([np.concatenate([re, -im], 1), np.concatenate([im, re], 1)], 0)

def setup_inputs():
    sw, ss = mx_kscale(KW), mx_kscale(KS)
    weak_t = np.random.randn(KW, P) / np.sqrt(2 * KW)
    core_t = np.random.randn(KS, P) / np.sqrt(2 * KS)
    weak_field = field_rows(KW)
    core_field = field_rows(KS)
    weak_words, weak_scales = pack4(weak_t / sw[:, None])
    return {
        "weak_field": bf(weak_field * sw),
        "weak_words": weak_words,
        "weak_scales": weak_scales,
        "core_field": bf(core_field * ss),
        "core_t": bf(core_t / ss[:, None]),
        "gain": bf(np.exp(0.6 * np.random.randn(P))),
    }

def reference(weak_field, weak_words, weak_scales, core_field, core_t, gain):
    a = mxq(f64(weak_field), 1, "e4m3")
    w = unpack4(weak_words, weak_scales)
    c = mxq(f64(core_field), 1, "e4m3")
    d = mxq(f64(core_t), 0, "e4m3")
    z = (a @ w) + (c @ d)
    z2 = z * z
    y = (z2[:F] + z2[F:]) * f64(gain)
    Y = y.T
    words, scales = planes(Y)
    return y, words, scales

@@ -1,0 +1,435 @@
+from contextlib import ExitStack
+
+import concourse.mybir as mybir
+from concourse.masks import make_identity
+
+F32 = mybir.dt.float32
+BF16 = mybir.dt.bfloat16
+I32 = mybir.dt.int32
+U32 = mybir.dt.uint32
+U8 = mybir.dt.uint8
+FP8X4 = mybir.dt.float8_e4m3fn_x4
+FP4X4 = mybir.dt.float4_e2m1fn_x4
+ALU = mybir.AluOpType
+SQUARE = mybir.ActivationFunctionType.Square
+
+FIELDS, PIXELS, K_WEAK, K_CORE = 512, 2048, 1536, 512
+FLOPS = 2 * (2 * FIELDS) * PIXELS * (K_WEAK + K_CORE)
+
+P = 128
+G = 512
+WEAK_PASSES = 3
+RE, IM = 0, 1
+
+
+def tile_lens_modes_pixel_intensity_g5_kernel(
+    tc, weak_field, weak_words, weak_scales, core_field, core_t, gain, out_0, out_1, out_2
+):
+    nc = tc.nc
+    with ExitStack() as ctx:
+        keep = ctx.enter_context(tc.tile_pool(name="keep", bufs=1))
+        work = ctx.enter_context(tc.tile_pool(name="work", bufs=4))
+        acc_pool = ctx.enter_context(tc.psum_pool(name="acc", bufs=5))
+        turn_pool = ctx.enter_context(tc.psum_pool(name="turn", bufs=3))
+        ctx.enter_context(tc.manual_schedule())
+
+        ident = keep.tile([P, P], F32, name="ident")
+        gain_rows = keep.tile([P, 16], BF16, name="gain_rows")
+        gain_all = keep.tile([P, PIXELS], BF16, name="gain_all")
+        table_warm = keep.tile([P, 1], F32, name="table_warm")
+        y_scales = keep.tile([P, 4, FIELDS], U8, name="y_scales", align_bytes=64)
+        y_codes = keep.tile([P, 4, FIELDS], U32, name="y_codes", align_bytes=64)
+        t = {}
+
+        def load_fields(i, part):
+            rows = slice(part * FIELDS + i * P, part * FIELDS + (i + 1) * P)
+            raw = keep.tile([P, K_WEAK + K_CORE], BF16, name="a_raw_%d_%d" % (i, part))
+            nc.sync.dma_start(out=raw[:, :K_WEAK], in_=weak_field[rows, :])
+            nc.sync.dma_start(out=raw[:, K_WEAK:], in_=core_field[rows, :])
+            t["a_raw", i, part] = raw
+
+        def load_w(g):
+            words = keep.tile([P, WEAK_PASSES, 2 * G], U8, name="w_words_%d" % g, align_bytes=64)
+            src = weak_words[:, :, 2 * G * g : 2 * G * (g + 1)].bitcast(I32)
+            nc.sync.dma_start(out=words[:].bitcast(I32), in_=src.rearrange("k p n -> p k n"))
+            t["w", g] = words
+
+        def load_d(g):
+            raw = keep.tile([P, 4, G], BF16, name="d_raw_%d" % g)
+            nc.sync.dma_start(out=raw[:], in_=core_t[:, G * g : G * (g + 1)].rearrange("(p j) n -> p j n", j=4))
+            t["d_raw", g] = raw
+
+        def group_d(g):
+            grouped = work.tile([P, G, 4], BF16, name="d_grouped", bufs=2, align_bytes=64)
+            nc.vector.tensor_copy(
+                out=grouped[:].rearrange("p (c i) j -> p c j i", i=4),
+                in_=t["d_raw", g][:].rearrange("p j (c i) -> p c j i", i=4),
+            )
+            t["d_grouped", g] = grouped
+
+        def quantize_d(g):
+            codes = keep.tile([P, G], U32, name="d_codes_%d" % g, align_bytes=64)
+            scales = keep.tile([P, G], U8, name="d_scales_%d" % g, align_bytes=64)
+            nc.vector.quantize_mx(
+                out=codes[:].bitcast(FP8X4), scales=scales[:], in_=t["d_grouped", g][:].rearrange("p n j -> p (n j)")
+            )
+            t["d", g] = (codes, scales)
+
+        def turn_fields(i, part, h):
+            bank = turn_pool.tile([P, 2, 2, P], F32, name="turn")
+            words = t["a_raw", i, part][:].bitcast(F32)
+            for k in range(2):
+                for u in range(2):
+                    first = 256 * (2 * h + k)
+                    nc.tensor.transpose(bank[:, k, u, :], words[:, first + u : first + 256 : 2], ident[:])
+            t["a_bank", i, part, h] = bank
+
+        def group_fields(i, part, h):
+            grouped = work.tile([P, 2, P, 4], BF16, name="a_grouped", align_bytes=64)
+            nc.scalar.copy(
+                out=grouped[:].bitcast(F32), in_=t["a_bank", i, part, h][:].rearrange("p k u f -> p k f u")
+            )
+            t["a_grouped", i, part, h] = grouped
+
+        def quantize_fields(i, part, h):
+            codes = keep.tile([P, 2 * P], U32, name="a_codes_%d_%d_%d" % (i, part, h), align_bytes=64)
+            scales = keep.tile([P, 2 * P], U8, name="a_scales_%d_%d_%d" % (i, part, h), align_bytes=64)
+            nc.vector.quantize_mx(
+                out=codes[:].bitcast(FP8X4),
+                scales=scales[:],
+                in_=t["a_grouped", i, part, h][:].rearrange("p k f t -> p (k f t)"),
+            )
+            t["a", i, part, h] = (codes, scales)
+
+        def multiply(i, part, g, passes, first=0, width=G):
+            pixels = slice(first, first + width)
+            for k in passes:
+                if k == 0:
+                    t["acc", i, part, g] = acc_pool.tile([P, width], F32, name="acc")
+                codes, scales = t["a", i, part, k // 2]
+                cols = slice(P * (k % 2), P * (k % 2 + 1))
+                if k < WEAK_PASSES:
+                    rhs = t["w", g][:, k, 2 * first : 2 * (first + width)].bitcast(FP4X4)
+                    start_col = G * (g % 2) + first
+                    rhs_scale = t["w_scales", g // 2][:, k, start_col : start_col + width]
+                else:
+                    rhs = t["d", g][0][:, pixels].bitcast(FP8X4)
+                    rhs_scale = t["d", g][1][:, pixels]
+                nc.tensor.matmul_mx(
+                    out=t["acc", i, part, g][:],
+                    lhsT=codes[:, cols].bitcast(FP8X4),
+                    lhsT_scale=scales[:, cols],
+                    rhs=rhs,
+                    rhs_scale=rhs_scale,
+                    start=(k == 0),
+                    stop=(k == WEAK_PASSES),
+                )
+
+        def square(i, part, g):
+            sq = work.tile([P, G], F32, name="sq", bufs=6)
+            nc.scalar.activation(out=sq[:], in_=t["acc", i, part, g][:], func=SQUARE)
+            t["sq", i, part, g] = sq
+
+        def add_squares(i, g):
+            total = work.tile([P, G], F32, name="total", bufs=3)
+            nc.vector.tensor_tensor(out=total[:], in0=t["sq", i, RE, g][:], in1=t["sq", i, IM, g][:], op=ALU.add)
+            t["total", i, g] = total
+
+        def apply_gain(i, g):
+            y = work.tile([P, G], F32, name="y", bufs=6)
+            nc.vector.tensor_tensor(
+                out=y[:], in0=t["total", i, g][:], in1=gain_all[:, G * g : G * (g + 1)], op=ALU.mult
+            )
+            nc.sync.dma_start(out=out_0[P * i : P * (i + 1), G * g : G * (g + 1)], in_=y[:])
+            t["y", i, g] = y
+
+        def round_y(i, g):
+            pairs = work.tile([P, 2, P, 2], BF16, name="y_pairs", bufs=6)
+            nc.vector.tensor_copy(out=pairs[:], in_=t["y", i, g][:].rearrange("f (p u e) -> f u p e", u=2, e=2))
+            t["y_pairs", i, g] = pairs
+
+        def turn_y(tiles, g):
+            bank = turn_pool.tile([P, len(tiles), 2, P], F32, name="turn")
+            for n, i in enumerate(tiles):
+                words = t["y_pairs", i, g][:].rearrange("f u p e -> f u (p e)").bitcast(F32)
+                for u in range(2):
+                    nc.tensor.transpose(bank[:, n, u, :], words[:, u, :], ident[:])
+            t["y_bank", tiles, g] = bank
+
+        def group_y(tiles, g):
+            grouped = work.tile([P, len(tiles), P, 4], BF16, name="y_grouped", bufs=4, align_bytes=64)
+            nc.scalar.copy(
+                out=grouped[:].bitcast(F32), in_=t["y_bank", tiles, g][:].rearrange("p n u f -> p n f u")
+            )
+            t["y_grouped", tiles, g] = grouped
+
+        def quantize_y(tiles, g):
+            cols = slice(P * tiles[0], P * (tiles[-1] + 1))
+            nc.vector.quantize_mx(
+                out=y_codes[:, g, cols].bitcast(FP8X4),
+                scales=y_scales[:, g, cols],
+                in_=t["y_grouped", tiles, g][:].rearrange("p n f t -> p (n f t)"),
+            )
+            if tiles[-1] % 2:
+                half = slice(P * (tiles[-1] - 1), P * (tiles[-1] + 1))
+                dst = out_1[g, :, half, :].rearrange("p m t -> p (m t)").bitcast(I32)
+                nc.sync.dma_start(out=dst, in_=y_codes[:, g, half].bitcast(I32))
+
+        def clear_w_scales(half):
+            plane = keep.tile([P, WEAK_PASSES, 2 * G], U8, name="w_scales_%d" % half, align_bytes=64)
+            nc.vector.memset(plane[:].bitcast(I32), 0)
+            t["w_scales", half] = plane
+
+        def load_w_scales(half):
+            for q in range(4):
+                src = weak_scales[:, 4 * q : 4 * q + 4, 2 * G * half : 2 * G * (half + 1)].bitcast(I32)
+                dst = t["w_scales", half][32 * q : 32 * q + 4, :, :].bitcast(I32)
+                nc.sync.dma_start(out=dst, in_=src.rearrange("k r n -> r k n"))
+
+        warm_in = keep.tile([P, 4 * P], BF16, name="warm_in", align_bytes=64)
+        warm_codes = keep.tile([P, P], U32, name="warm_codes", align_bytes=64)
+        warm_scales = keep.tile([P, P], U8, name="warm_scales", align_bytes=64)
+
+        def warm(count):
+            warm_acc = acc_pool.tile([P, P], F32, name="acc")
+            for n in range(count):
+                nc.tensor.matmul_mx(
+                    out=warm_acc[:],
+                    lhsT=warm_codes[:].bitcast(FP8X4),
+                    lhsT_scale=warm_scales[:],
+                    rhs=warm_codes[:].bitcast(FP8X4),
+                    rhs_scale=warm_scales[:],
+                    start=True,
+                    stop=True,
+                )
+
+        def spread_gain():
+            gain_words = gain_rows[:].bitcast(F32)
+            all_words = gain_all[:].bitcast(F32).rearrange("p (n c) -> p n c", c=8)
+            for b in range(2):
+                bank = turn_pool.tile([P, 4, P], F32, name="turn")
+                for c in range(4):
+                    column = gain_words[:, 4 * b + c : 4 * b + c + 1]
+                    nc.tensor.transpose(bank[:, c, :], column.to_broadcast([P, P]), ident[:])
+                nc.scalar.copy(out=all_words[:, :, 4 * b : 4 * b + 4], in_=bank[:].rearrange("p c n -> p n c"))
+
+        def prepare_fields(i, part):
+            for h in range(2):
+                turn_fields(i, part, h)
+            for h in range(2):
+                group_fields(i, part, h)
+
+        def quantize_both(i, part):
+            for h in range(2):
+                quantize_fields(i, part, h)
+
+        weak = range(WEAK_PASSES)
+        core = [WEAK_PASSES]
+        every = range(WEAK_PASSES + 1)
+
+        def product(i, part, g, passes):
+            multiply(i, part, g, passes)
+            square(i, part, g)
+
+        def products(i, g):
+            for part in (RE, IM):
+                product(i, part, g, every)
+
+        def finish(i, g):
+            add_squares(i, g)
+            apply_gain(i, g)
+            round_y(i, g)
+
+        def fields(i, part):
+            prepare_fields(i, part)
+            quantize_both(i, part)
+
+        def turn_planes(*units):
+            for unit in units:
+                turn_y(*unit)
+            for unit in units:
+                group_y(*unit)
+
+        def planes(*units):
+            turn_planes(*units)
+            for unit in units:
+                quantize_y(*unit)
+
+        def core_operand(g):
+            group_d(g)
+            quantize_d(g)
+
+        def tile(i, g):
+            products(i, g)
+            finish(i, g)
+
+        nc.sync.dma_start(out=gain_rows[:], in_=gain.rearrange("(p c) -> p c", p=P))
+        nc.vector.memset(warm_in[:], 1.0)
+        clear_w_scales(0)
+        nc.vector.quantize_mx(out=warm_codes[:].bitcast(FP8X4), scales=warm_scales[:], in_=warm_in[:])
+        clear_w_scales(1)
+        nc.scalar.activation(out=table_warm[:], in_=warm_in[:, 0:1], func=SQUARE)
+        make_identity(nc, ident[:])
+        load_fields(0, RE)
+        load_w_scales(0)
+        load_w(0)
+        load_fields(0, IM)
+        load_w(1)
+        load_d(0)
+        load_fields(1, RE)
+        load_d(1)
+        load_fields(1, IM)
+        load_w_scales(1)
+        load_w(2)
+        load_d(2)
+        load_fields(2, RE)
+        load_w(3)
+        load_d(3)
+        load_fields(2, IM)
+        load_fields(3, RE)
+        load_fields(3, IM)
+
+        warm(14)
+        fields(0, RE)
+        spread_gain()
+        warm(4)
+        multiply(0, RE, 0, weak)
+        fields(0, IM)
+        multiply(0, RE, 1, weak)
+        group_d(0)
+        prepare_fields(1, RE)
+        quantize_d(0)
+        multiply(0, IM, 0, weak)
+        quantize_both(1, RE)
+        multiply(0, IM, 1, weak)
+        group_d(1)
+        product(0, RE, 0, core)
+        product(0, IM, 0, core)
+        quantize_d(1)
+        multiply(1, RE, 0, every)
+        prepare_fields(1, IM)
+        square(1, RE, 0)
+        add_squares(0, 0)
+        quantize_both(1, IM)
+        product(0, RE, 1, core)
+        product(0, IM, 1, core)
+        apply_gain(0, 0)
+        group_d(2)
+        product(1, RE, 1, every)
+        round_y(0, 0)
+        quantize_d(2)
+        add_squares(0, 1)
+        product(1, IM, 0, every)
+        apply_gain(0, 1)
+        add_squares(1, 0)
+        round_y(0, 1)
+        apply_gain(1, 0)
+        multiply(1, IM, 1, every)
+        prepare_fields(2, RE)
+        square(1, IM, 1)
+        group_d(3)
+        round_y(1, 0)
+        quantize_d(3)
+        add_squares(1, 1)
+        quantize_both(2, RE)
+        apply_gain(1, 1)
+        products(0, 2)
+        add_squares(0, 2)
+        round_y(1, 1)
+        apply_gain(0, 2)
+        products(1, 2)
+        add_squares(1, 2)
+        round_y(0, 2)
+        apply_gain(1, 2)
+        prepare_fields(2, IM)
+        turn_planes(((0, 1), 0))
+        quantize_both(2, IM)
+        products(0, 3)
+        quantize_y((0, 1), 0)
+        add_squares(0, 3)
+        round_y(1, 2)
+        apply_gain(0, 3)
+        prepare_fields(3, RE)
+        turn_planes(((0, 1), 1))
+        quantize_both(3, RE)
+        products(1, 3)
+        quantize_y((0, 1), 1)
+        add_squares(1, 3)
+        round_y(0, 3)
+        apply_gain(1, 3)
+        prepare_fields(3, IM)
+        turn_planes(((0, 1), 2))
+        quantize_both(3, IM)
+        products(2, 0)
+        quantize_y((0, 1), 2)
+        add_squares(2, 0)
+        round_y(1, 3)
+        apply_gain(2, 0)
+        products(3, 0)
+        add_squares(3, 0)
+        round_y(2, 0)
+        apply_gain(3, 0)
+        products(2, 1)
+        add_squares(2, 1)
+        round_y(3, 0)
+        apply_gain(2, 1)
+        products(3, 1)
+        add_squares(3, 1)
+        round_y(2, 1)
+        apply_gain(3, 1)
+        turn_planes(((0, 1), 3), ((2, 3), 0))
+        products(2, 2)
+        quantize_y((0, 1), 3)
+        quantize_y((2, 3), 0)
+        add_squares(2, 2)
+        round_y(3, 1)
+        apply_gain(2, 2)
+        products(3, 2)
+        round_y(2, 2)
+        finish(3, 2)
+        products(2, 3)
+        turn_planes(((2, 3), 1), ((2,), 2))
+        add_squares(2, 3)
+        quantize_y((2, 3), 1)
+        apply_gain(2, 3)
+        quantize_y((2,), 2)
+        round_y(2, 3)
+
+        i, g = 3, 3
+        product(i, RE, g, every)
+        total = work.tile([P, G], F32, name="total", bufs=3)
+        pairs = work.tile([P, 2, P, 2], BF16, name="y_pairs", bufs=6)
+        t["total", i, g] = total
+        t["y_pairs", i, g] = pairs
+        chunks = 4
+        width = G // chunks
+
+        def gain_chunk(c):
+            words = slice(c * width // 4, (c + 1) * width // 4)
+            pixels = slice(c * width, (c + 1) * width)
+            nc.vector.tensor_tensor(
+                out=pairs[:, :, words, :],
+                in0=total[:, pixels].rearrange("f (p u e) -> f u p e", u=2, e=2),
+                in1=gain_all[:, G * g : G * (g + 1)][:, pixels].rearrange("f (p u e) -> f u p e", u=2, e=2),
+                op=ALU.mult,
+            )
+
+        for c in range(chunks):
+            pixels = slice(c * width, (c + 1) * width)
+            multiply(i, IM, g, every, c * width, width)
+            sq = work.tile([P, width], F32, name="sq_chunk")
+            nc.scalar.activation(out=sq[:], in_=t["acc", i, IM, g][:], func=SQUARE)
+            nc.vector.tensor_tensor(out=total[:, pixels], in0=t["sq", i, RE, g][:, pixels], in1=sq[:], op=ALU.add)
+            if c > 0:
+                gain_chunk(c - 1)
+        gain_chunk(chunks - 1)
+        turn_planes(((3,), 2), ((2,), 3))
+        apply_gain(3, 3)
+        turn_planes(((3,), 3))
+        quantize_y((3,), 2)
+        quantize_y((2,), 3)
+        quantize_y((3,), 3)
+        for q in range(4):
+            dst = out_2[:, 4 * q : 4 * q + 4, :].bitcast(I32).rearrange("g r m -> r g m")
+            queue = nc.scalar if q % 2 else nc.sync
+            queue.dma_start(out=dst, in_=y_scales[32 * q : 32 * q + 4, :, :].bitcast(I32))

@@ -20,6 +20,7 @@ P = 128
 G = 512
 WEAK_PASSES = 3
 RE, IM = 0, 1
+SCALE_LOADS = ((0, 1), (1, 1), (2, 2))
 
 
 def tile_lens_modes_pixel_intensity_g5_kernel(
@@ -29,7 +30,7 @@ def tile_lens_modes_pixel_intensity_g5_kernel(
     with ExitStack() as ctx:
         keep = ctx.enter_context(tc.tile_pool(name="keep", bufs=1))
         work = ctx.enter_context(tc.tile_pool(name="work", bufs=4))
-        acc_pool = ctx.enter_context(tc.psum_pool(name="acc", bufs=5))
+        acc_pool = ctx.enter_context(tc.psum_pool(name="acc", bufs=1))
         turn_pool = ctx.enter_context(tc.psum_pool(name="turn", bufs=3))
         ctx.enter_context(tc.manual_schedule())
 
@@ -40,6 +41,7 @@ def tile_lens_modes_pixel_intensity_g5_kernel(
         y_scales = keep.tile([P, 4, FIELDS], U8, name="y_scales", align_bytes=64)
         y_codes = keep.tile([P, 4, FIELDS], U32, name="y_codes", align_bytes=64)
         t = {}
+        free_banks = ["acc_%d" % n for n in range(5)]
 
         def load_fields(i, part):
             rows = slice(part * FIELDS + i * P, part * FIELDS + (i + 1) * P)
@@ -75,13 +77,30 @@ def tile_lens_modes_pixel_intensity_g5_kernel(
             )
             t["d", g] = (codes, scales)
 
+        def split_words(i, part):
+            split = work.tile([P, 4, 2, P], F32, name="a_split", bufs=2)
+            words = t["a_raw", i, part][:].bitcast(F32)
+            nc.scalar.copy(out=split[:], in_=words.rearrange("f (k p u) -> f k u p", k=4, u=2))
+            t["a_split", i, part] = split
+
+        def store_y_scales(half):
+            groups = slice(2 * half, 2 * half + 2)
+            for q in range(4):
+                dst = out_2[groups, 4 * q : 4 * q + 4, :].bitcast(I32).rearrange("g r m -> r g m")
+                queue = nc.scalar if half and q % 2 else nc.sync
+                queue.dma_start(out=dst, in_=y_scales[32 * q : 32 * q + 4, groups, :].bitcast(I32))
+
         def turn_fields(i, part, h):
             bank = turn_pool.tile([P, 2, 2, P], F32, name="turn")
             words = t["a_raw", i, part][:].bitcast(F32)
             for k in range(2):
                 for u in range(2):
                     first = 256 * (2 * h + k)
-                    nc.tensor.transpose(bank[:, k, u, :], words[:, first + u : first + 256 : 2], ident[:])
+                    if ("a_split", i, part) in t:
+                        source = t["a_split", i, part][:, 2 * h + k, u, :]
+                    else:
+                        source = words[:, first + u : first + 256 : 2]
+                    nc.tensor.transpose(bank[:, k, u, :], source, ident[:])
             t["a_bank", i, part, h] = bank
 
         def group_fields(i, part, h):
@@ -105,13 +124,13 @@ def tile_lens_modes_pixel_intensity_g5_kernel(
             pixels = slice(first, first + width)
             for k in passes:
                 if k == 0:
-                    t["acc", i, part, g] = acc_pool.tile([P, width], F32, name="acc")
+                    t["bank", i, part, g] = free_banks.pop(0)
+                    t["acc", i, part, g] = acc_pool.tile([P, width], F32, name=t["bank", i, part, g])
                 codes, scales = t["a", i, part, k // 2]
                 cols = slice(P * (k % 2), P * (k % 2 + 1))
                 if k < WEAK_PASSES:
                     rhs = t["w", g][:, k, 2 * first : 2 * (first + width)].bitcast(FP4X4)
-                    start_col = G * (g % 2) + first
-                    rhs_scale = t["w_scales", g // 2][:, k, start_col : start_col + width]
+                    rhs_scale = t["w_scales", g][:, k, pixels]
                 else:
                     rhs = t["d", g][0][:, pixels].bitcast(FP8X4)
                     rhs_scale = t["d", g][1][:, pixels]
@@ -129,6 +148,7 @@ def tile_lens_modes_pixel_intensity_g5_kernel(
             sq = work.tile([P, G], F32, name="sq", bufs=6)
             nc.scalar.activation(out=sq[:], in_=t["acc", i, part, g][:], func=SQUARE)
             t["sq", i, part, g] = sq
+            free_banks.append(t["bank", i, part, g])
 
         def add_squares(i, g):
             total = work.tile([P, G], F32, name="total", bufs=3)
@@ -175,15 +195,17 @@ def tile_lens_modes_pixel_intensity_g5_kernel(
                 dst = out_1[g, :, half, :].rearrange("p m t -> p (m t)").bitcast(I32)
                 nc.sync.dma_start(out=dst, in_=y_codes[:, g, half].bitcast(I32))
 
-        def clear_w_scales(half):
-            plane = keep.tile([P, WEAK_PASSES, 2 * G], U8, name="w_scales_%d" % half, align_bytes=64)
+        def clear_w_scales(first, count):
+            plane = keep.tile([P, WEAK_PASSES, count * G], U8, name="w_scales_%d" % first, align_bytes=64)
             nc.vector.memset(plane[:].bitcast(I32), 0)
-            t["w_scales", half] = plane
+            t["w_plane", first] = plane
+            for n in range(count):
+                t["w_scales", first + n] = plane[:, :, G * n : G * (n + 1)]
 
-        def load_w_scales(half):
+        def load_w_scales(first, count):
             for q in range(4):
-                src = weak_scales[:, 4 * q : 4 * q + 4, 2 * G * half : 2 * G * (half + 1)].bitcast(I32)
-                dst = t["w_scales", half][32 * q : 32 * q + 4, :, :].bitcast(I32)
+                src = weak_scales[:, 4 * q : 4 * q + 4, G * first : G * (first + count)].bitcast(I32)
+                dst = t["w_plane", first][32 * q : 32 * q + 4, :, :].bitcast(I32)
                 nc.sync.dma_start(out=dst, in_=src.rearrange("k r n -> r k n"))
 
         warm_in = keep.tile([P, 4 * P], BF16, name="warm_in", align_bytes=64)
@@ -191,7 +213,7 @@ def tile_lens_modes_pixel_intensity_g5_kernel(
         warm_scales = keep.tile([P, P], U8, name="warm_scales", align_bytes=64)
 
         def warm(count):
-            warm_acc = acc_pool.tile([P, P], F32, name="acc")
+            warm_acc = acc_pool.tile([P, P], F32, name=free_banks[-1])
             for n in range(count):
                 nc.tensor.matmul_mx(
                     out=warm_acc[:],
@@ -263,80 +285,84 @@ def tile_lens_modes_pixel_intensity_g5_kernel(
             products(i, g)
             finish(i, g)
 
-        nc.sync.dma_start(out=gain_rows[:], in_=gain.rearrange("(p c) -> p c", p=P))
-        nc.vector.memset(warm_in[:], 1.0)
-        clear_w_scales(0)
+        nc.gpsimd.memset(warm_in[:], 1.0)
         nc.vector.quantize_mx(out=warm_codes[:].bitcast(FP8X4), scales=warm_scales[:], in_=warm_in[:])
-        clear_w_scales(1)
+        for first, count in SCALE_LOADS:
+            clear_w_scales(first, count)
         nc.scalar.activation(out=table_warm[:], in_=warm_in[:, 0:1], func=SQUARE)
         make_identity(nc, ident[:])
         load_fields(0, RE)
-        load_w_scales(0)
         load_w(0)
+        nc.sync.dma_start(out=gain_rows[:], in_=gain.rearrange("(p c) -> p c", p=P))
+        load_w_scales(0, 1)
         load_fields(0, IM)
         load_w(1)
-        load_d(0)
+        load_w_scales(1, 1)
         load_fields(1, RE)
-        load_d(1)
+        load_d(0)
         load_fields(1, IM)
-        load_w_scales(1)
+        load_d(1)
+        load_w_scales(2, 2)
         load_w(2)
         load_d(2)
         load_fields(2, RE)
+        load_fields(2, IM)
         load_w(3)
         load_d(3)
-        load_fields(2, IM)
         load_fields(3, RE)
         load_fields(3, IM)
 
-        warm(14)
+        warm(16)
         fields(0, RE)
+        warm(5)
         spread_gain()
-        warm(4)
         multiply(0, RE, 0, weak)
         fields(0, IM)
         multiply(0, RE, 1, weak)
-        group_d(0)
         prepare_fields(1, RE)
+        group_d(0)
+        quantize_both(1, RE)
         quantize_d(0)
         multiply(0, IM, 0, weak)
-        quantize_both(1, RE)
         multiply(0, IM, 1, weak)
         group_d(1)
-        product(0, RE, 0, core)
-        product(0, IM, 0, core)
-        quantize_d(1)
-        multiply(1, RE, 0, every)
         prepare_fields(1, IM)
-        square(1, RE, 0)
+        quantize_fields(1, IM, 0)
+        quantize_d(1)
+        quantize_fields(1, IM, 1)
+        product(0, RE, 0, core)
+        multiply(1, RE, 0, weak)
+        product(0, IM, 0, core)
+        product(1, RE, 0, core)
+        group_d(2)
+        product(1, IM, 0, every)
         add_squares(0, 0)
-        quantize_both(1, IM)
+        quantize_d(2)
         product(0, RE, 1, core)
         product(0, IM, 1, core)
         apply_gain(0, 0)
-        group_d(2)
-        product(1, RE, 1, every)
-        round_y(0, 0)
-        quantize_d(2)
-        add_squares(0, 1)
-        product(1, IM, 0, every)
-        apply_gain(0, 1)
         add_squares(1, 0)
-        round_y(0, 1)
+        round_y(0, 0)
         apply_gain(1, 0)
-        multiply(1, IM, 1, every)
-        prepare_fields(2, RE)
-        square(1, IM, 1)
-        group_d(3)
+        add_squares(0, 1)
         round_y(1, 0)
-        quantize_d(3)
+        apply_gain(0, 1)
+        product(1, RE, 1, every)
+        split_words(2, RE)
+        product(1, IM, 1, every)
+        group_d(3)
         add_squares(1, 1)
-        quantize_both(2, RE)
+        quantize_d(3)
+        round_y(0, 1)
         apply_gain(1, 1)
-        products(0, 2)
+        product(0, RE, 2, every)
+        split_words(2, IM)
+        product(0, IM, 2, every)
         add_squares(0, 2)
         round_y(1, 1)
         apply_gain(0, 2)
+        prepare_fields(2, RE)
+        quantize_both(2, RE)
         products(1, 2)
         add_squares(1, 2)
         round_y(0, 2)
@@ -349,51 +375,59 @@ def tile_lens_modes_pixel_intensity_g5_kernel(
         add_squares(0, 3)
         round_y(1, 2)
         apply_gain(0, 3)
-        prepare_fields(3, RE)
-        turn_planes(((0, 1), 1))
-        quantize_both(3, RE)
         products(1, 3)
-        quantize_y((0, 1), 1)
         add_squares(1, 3)
         round_y(0, 3)
         apply_gain(1, 3)
-        prepare_fields(3, IM)
-        turn_planes(((0, 1), 2))
-        quantize_both(3, IM)
-        products(2, 0)
-        quantize_y((0, 1), 2)
+        product(2, RE, 0, every)
+        split_words(3, RE)
+        product(2, IM, 0, every)
         add_squares(2, 0)
         round_y(1, 3)
         apply_gain(2, 0)
+        product(2, RE, 1, every)
+        split_words(3, IM)
+        product(2, IM, 1, every)
+        add_squares(2, 1)
+        round_y(2, 0)
+        apply_gain(2, 1)
+        prepare_fields(3, RE)
+        turn_planes(((0, 1), 1))
+        quantize_both(3, RE)
+        products(2, 2)
+        quantize_y((0, 1), 1)
+        add_squares(2, 2)
+        round_y(2, 1)
+        apply_gain(2, 2)
+        prepare_fields(3, IM)
+        turn_planes(((0, 1), 2))
+        quantize_both(3, IM)
+        products(2, 3)
+        quantize_y((0, 1), 2)
+        add_squares(2, 3)
+        round_y(2, 2)
+        apply_gain(2, 3)
         products(3, 0)
         add_squares(3, 0)
-        round_y(2, 0)
+        round_y(2, 3)
         apply_gain(3, 0)
-        products(2, 1)
-        add_squares(2, 1)
-        round_y(3, 0)
-        apply_gain(2, 1)
         products(3, 1)
         add_squares(3, 1)
-        round_y(2, 1)
+        round_y(3, 0)
         apply_gain(3, 1)
-        turn_planes(((0, 1), 3), ((2, 3), 0))
-        products(2, 2)
+        turn_planes(((0, 1), 3), ((2,), 2), ((2,), 3))
         quantize_y((0, 1), 3)
-        quantize_y((2, 3), 0)
-        add_squares(2, 2)
         round_y(3, 1)
-        apply_gain(2, 2)
-        products(3, 2)
-        round_y(2, 2)
-        finish(3, 2)
-        products(2, 3)
-        turn_planes(((2, 3), 1), ((2,), 2))
-        add_squares(2, 3)
-        quantize_y((2, 3), 1)
-        apply_gain(2, 3)
         quantize_y((2,), 2)
-        round_y(2, 3)
+        quantize_y((2,), 3)
+        products(3, 2)
+        turn_planes(((2, 3), 0), ((2, 3), 1))
+        add_squares(3, 2)
+        quantize_y((2, 3), 0)
+        apply_gain(3, 2)
+        quantize_y((2, 3), 1)
+        store_y_scales(0)
+        round_y(3, 2)
 
         i, g = 3, 3
         product(i, RE, g, every)
@@ -419,17 +453,14 @@ def tile_lens_modes_pixel_intensity_g5_kernel(
             multiply(i, IM, g, every, c * width, width)
             sq = work.tile([P, width], F32, name="sq_chunk")
             nc.scalar.activation(out=sq[:], in_=t["acc", i, IM, g][:], func=SQUARE)
+            free_banks.append(t["bank", i, IM, g])
             nc.vector.tensor_tensor(out=total[:, pixels], in0=t["sq", i, RE, g][:, pixels], in1=sq[:], op=ALU.add)
             if c > 0:
                 gain_chunk(c - 1)
         gain_chunk(chunks - 1)
-        turn_planes(((3,), 2), ((2,), 3))
+        turn_planes(((3,), 2))
         apply_gain(3, 3)
         turn_planes(((3,), 3))
         quantize_y((3,), 2)
-        quantize_y((2,), 3)
         quantize_y((3,), 3)
-        for q in range(4):
-            dst = out_2[:, 4 * q : 4 * q + 4, :].bitcast(I32).rearrange("g r m -> r g m")
-            queue = nc.scalar if q % 2 else nc.sync
-            queue.dma_start(out=dst, in_=y_scales[32 * q : 32 * q + 4, :, :].bitcast(I32))
+        store_y_scales(1)

@@ -20,7 +20,7 @@ P = 128
 G = 512
 WEAK_PASSES = 3
 RE, IM = 0, 1
-SCALE_LOADS = ((0, 1), (1, 1), (2, 2))
+SCALE_LOADS = ((0, 2), (2, 2))
 
 
 def tile_lens_modes_pixel_intensity_g5_kernel(
@@ -31,7 +31,6 @@ def tile_lens_modes_pixel_intensity_g5_kernel(
         keep = ctx.enter_context(tc.tile_pool(name="keep", bufs=1))
         work = ctx.enter_context(tc.tile_pool(name="work", bufs=4))
         acc_pool = ctx.enter_context(tc.psum_pool(name="acc", bufs=1))
-        turn_pool = ctx.enter_context(tc.psum_pool(name="turn", bufs=3))
         ctx.enter_context(tc.manual_schedule())
 
         ident = keep.tile([P, P], F32, name="ident")
@@ -41,7 +40,7 @@ def tile_lens_modes_pixel_intensity_g5_kernel(
         y_scales = keep.tile([P, 4, FIELDS], U8, name="y_scales", align_bytes=64)
         y_codes = keep.tile([P, 4, FIELDS], U32, name="y_codes", align_bytes=64)
         t = {}
-        free_banks = ["acc_%d" % n for n in range(5)]
+        free_banks = ["acc_%d" % n for n in range(8)]
 
         def load_fields(i, part):
             rows = slice(part * FIELDS + i * P, part * FIELDS + (i + 1) * P)
@@ -84,14 +83,15 @@ def tile_lens_modes_pixel_intensity_g5_kernel(
             t["a_split", i, part] = split
 
         def store_y_scales(half):
-            groups = slice(2 * half, 2 * half + 2)
+            cols = slice(2 * P * half, 2 * P * (half + 1))
             for q in range(4):
-                dst = out_2[groups, 4 * q : 4 * q + 4, :].bitcast(I32).rearrange("g r m -> r g m")
+                dst = out_2[:, 4 * q : 4 * q + 4, cols].bitcast(I32).rearrange("g r m -> r g m")
                 queue = nc.scalar if half and q % 2 else nc.sync
-                queue.dma_start(out=dst, in_=y_scales[32 * q : 32 * q + 4, groups, :].bitcast(I32))
+                queue.dma_start(out=dst, in_=y_scales[32 * q : 32 * q + 4, :, cols].bitcast(I32))
 
         def turn_fields(i, part, h):
-            bank = turn_pool.tile([P, 2, 2, P], F32, name="turn")
+            t["a_bank_name", i, part, h] = free_banks.pop(0)
+            bank = acc_pool.tile([P, 2, 2, P], F32, name=t["a_bank_name", i, part, h])
             words = t["a_raw", i, part][:].bitcast(F32)
             for k in range(2):
                 for u in range(2):
@@ -104,11 +104,12 @@ def tile_lens_modes_pixel_intensity_g5_kernel(
             t["a_bank", i, part, h] = bank
 
         def group_fields(i, part, h):
-            grouped = work.tile([P, 2, P, 4], BF16, name="a_grouped", align_bytes=64)
+            grouped = work.tile([P, 2, P, 4], BF16, name="a_grouped", bufs=5, align_bytes=64)
             nc.scalar.copy(
                 out=grouped[:].bitcast(F32), in_=t["a_bank", i, part, h][:].rearrange("p k u f -> p k f u")
             )
             t["a_grouped", i, part, h] = grouped
+            free_banks.append(t["a_bank_name", i, part, h])
 
         def quantize_fields(i, part, h):
             codes = keep.tile([P, 2 * P], U32, name="a_codes_%d_%d_%d" % (i, part, h), align_bytes=64)
@@ -164,12 +165,13 @@ def tile_lens_modes_pixel_intensity_g5_kernel(
             t["y", i, g] = y
 
         def round_y(i, g):
-            pairs = work.tile([P, 2, P, 2], BF16, name="y_pairs", bufs=6)
+            pairs = work.tile([P, 2, P, 2], BF16, name="y_pairs", bufs=8)
             nc.vector.tensor_copy(out=pairs[:], in_=t["y", i, g][:].rearrange("f (p u e) -> f u p e", u=2, e=2))
             t["y_pairs", i, g] = pairs
 
         def turn_y(tiles, g):
-            bank = turn_pool.tile([P, len(tiles), 2, P], F32, name="turn")
+            t["y_bank_name", tiles, g] = free_banks.pop(0)
+            bank = acc_pool.tile([P, len(tiles), 2, P], F32, name=t["y_bank_name", tiles, g])
             for n, i in enumerate(tiles):
                 words = t["y_pairs", i, g][:].rearrange("f u p e -> f u (p e)").bitcast(F32)
                 for u in range(2):
@@ -177,11 +179,12 @@ def tile_lens_modes_pixel_intensity_g5_kernel(
             t["y_bank", tiles, g] = bank
 
         def group_y(tiles, g):
-            grouped = work.tile([P, len(tiles), P, 4], BF16, name="y_grouped", bufs=4, align_bytes=64)
+            grouped = work.tile([P, len(tiles), P, 4], BF16, name="y_grouped", bufs=5, align_bytes=64)
             nc.scalar.copy(
                 out=grouped[:].bitcast(F32), in_=t["y_bank", tiles, g][:].rearrange("p n u f -> p n f u")
             )
             t["y_grouped", tiles, g] = grouped
+            free_banks.append(t["y_bank_name", tiles, g])
 
         def quantize_y(tiles, g):
             cols = slice(P * tiles[0], P * (tiles[-1] + 1))
@@ -213,7 +216,7 @@ def tile_lens_modes_pixel_intensity_g5_kernel(
         warm_scales = keep.tile([P, P], U8, name="warm_scales", align_bytes=64)
 
         def warm(count):
-            warm_acc = acc_pool.tile([P, P], F32, name=free_banks[-1])
+            warm_acc = acc_pool.tile([P, P], F32, name=free_banks[0])
             for n in range(count):
                 nc.tensor.matmul_mx(
                     out=warm_acc[:],
@@ -229,17 +232,31 @@ def tile_lens_modes_pixel_intensity_g5_kernel(
             gain_words = gain_rows[:].bitcast(F32)
             all_words = gain_all[:].bitcast(F32).rearrange("p (n c) -> p n c", c=8)
             for b in range(2):
-                bank = turn_pool.tile([P, 4, P], F32, name="turn")
+                bank_name = free_banks.pop(0)
+                bank = acc_pool.tile([P, 4, P], F32, name=bank_name)
                 for c in range(4):
                     column = gain_words[:, 4 * b + c : 4 * b + c + 1]
                     nc.tensor.transpose(bank[:, c, :], column.to_broadcast([P, P]), ident[:])
-                nc.scalar.copy(out=all_words[:, :, 4 * b : 4 * b + 4], in_=bank[:].rearrange("p c n -> p n c"))
+                nc.vector.tensor_copy(out=all_words[:, :, 4 * b : 4 * b + 4], in_=bank[:].rearrange("p c n -> p n c"))
+                free_banks.append(bank_name)
 
         def prepare_fields(i, part):
             for h in range(2):
                 turn_fields(i, part, h)
             for h in range(2):
                 group_fields(i, part, h)
+
+        def turn_pair(i, *units):
+            for part in (RE, IM):
+                for h in range(2):
+                    turn_fields(i, part, h)
+            for unit in units:
+                turn_y(*unit)
+            for part in (RE, IM):
+                for h in range(2):
+                    group_fields(i, part, h)
+            for unit in units:
+                group_y(*unit)
 
         def quantize_both(i, part):
             for h in range(2):
@@ -285,34 +302,34 @@ def tile_lens_modes_pixel_intensity_g5_kernel(
             products(i, g)
             finish(i, g)
 
-        nc.gpsimd.memset(warm_in[:], 1.0)
+        nc.gpsimd.dma_start(out=gain_rows[:], in_=gain.rearrange("(p c) -> p c", p=P))
+        nc.vector.memset(warm_in[:], 1.0)
+        clear_w_scales(*SCALE_LOADS[0])
         nc.vector.quantize_mx(out=warm_codes[:].bitcast(FP8X4), scales=warm_scales[:], in_=warm_in[:])
-        for first, count in SCALE_LOADS:
+        for first, count in SCALE_LOADS[1:]:
             clear_w_scales(first, count)
         nc.scalar.activation(out=table_warm[:], in_=warm_in[:, 0:1], func=SQUARE)
         make_identity(nc, ident[:])
         load_fields(0, RE)
         load_w(0)
-        nc.sync.dma_start(out=gain_rows[:], in_=gain.rearrange("(p c) -> p c", p=P))
-        load_w_scales(0, 1)
+        load_w_scales(0, 2)
         load_fields(0, IM)
         load_w(1)
-        load_w_scales(1, 1)
         load_fields(1, RE)
         load_d(0)
         load_fields(1, IM)
         load_d(1)
+        load_d(2)
         load_w_scales(2, 2)
         load_w(2)
-        load_d(2)
         load_fields(2, RE)
         load_fields(2, IM)
-        load_w(3)
         load_d(3)
+        load_w(3)
         load_fields(3, RE)
         load_fields(3, IM)
 
-        warm(16)
+        warm(19)
         fields(0, RE)
         warm(5)
         spread_gain()
@@ -328,10 +345,10 @@ def tile_lens_modes_pixel_intensity_g5_kernel(
         group_d(1)
         prepare_fields(1, IM)
         quantize_fields(1, IM, 0)
-        quantize_d(1)
         quantize_fields(1, IM, 1)
-        product(0, RE, 0, core)
+        quantize_d(1)
         multiply(1, RE, 0, weak)
+        product(0, RE, 0, core)
         product(0, IM, 0, core)
         product(1, RE, 0, core)
         group_d(2)
@@ -361,21 +378,22 @@ def tile_lens_modes_pixel_intensity_g5_kernel(
         add_squares(0, 2)
         round_y(1, 1)
         apply_gain(0, 2)
-        prepare_fields(2, RE)
-        quantize_both(2, RE)
-        products(1, 2)
+        product(1, RE, 2, every)
+        product(1, IM, 2, every)
         add_squares(1, 2)
         round_y(0, 2)
         apply_gain(1, 2)
-        prepare_fields(2, IM)
-        turn_planes(((0, 1), 0))
+        turn_pair(2, ((0, 1), 0))
+        quantize_both(2, RE)
         quantize_both(2, IM)
-        products(0, 3)
+        product(0, RE, 3, every)
+        product(0, IM, 3, every)
         quantize_y((0, 1), 0)
         add_squares(0, 3)
         round_y(1, 2)
         apply_gain(0, 3)
-        products(1, 3)
+        product(1, RE, 3, every)
+        product(1, IM, 3, every)
         add_squares(1, 3)
         round_y(0, 3)
         apply_gain(1, 3)
@@ -391,33 +409,35 @@ def tile_lens_modes_pixel_intensity_g5_kernel(
         add_squares(2, 1)
         round_y(2, 0)
         apply_gain(2, 1)
-        prepare_fields(3, RE)
-        turn_planes(((0, 1), 1))
-        quantize_both(3, RE)
-        products(2, 2)
-        quantize_y((0, 1), 1)
+        product(2, RE, 2, every)
+        product(2, IM, 2, every)
         add_squares(2, 2)
         round_y(2, 1)
         apply_gain(2, 2)
-        prepare_fields(3, IM)
-        turn_planes(((0, 1), 2))
+        turn_pair(3, ((0, 1), 1))
+        quantize_both(3, RE)
         quantize_both(3, IM)
-        products(2, 3)
-        quantize_y((0, 1), 2)
+        product(2, RE, 3, every)
+        product(2, IM, 3, every)
+        quantize_y((0, 1), 1)
         add_squares(2, 3)
         round_y(2, 2)
         apply_gain(2, 3)
-        products(3, 0)
+        product(3, RE, 0, every)
+        product(3, IM, 0, every)
         add_squares(3, 0)
         round_y(2, 3)
         apply_gain(3, 0)
-        products(3, 1)
+        product(3, RE, 1, every)
+        product(3, IM, 1, every)
         add_squares(3, 1)
         round_y(3, 0)
         apply_gain(3, 1)
-        turn_planes(((0, 1), 3), ((2,), 2), ((2,), 3))
-        quantize_y((0, 1), 3)
+        turn_planes(((0, 1), 2), ((0, 1), 3), ((2,), 2), ((2,), 3))
         round_y(3, 1)
+        quantize_y((0, 1), 2)
+        quantize_y((0, 1), 3)
+        store_y_scales(0)
         quantize_y((2,), 2)
         quantize_y((2,), 3)
         products(3, 2)
@@ -426,13 +446,12 @@ def tile_lens_modes_pixel_intensity_g5_kernel(
         quantize_y((2, 3), 0)
         apply_gain(3, 2)
         quantize_y((2, 3), 1)
-        store_y_scales(0)
         round_y(3, 2)
 
         i, g = 3, 3
         product(i, RE, g, every)
         total = work.tile([P, G], F32, name="total", bufs=3)
-        pairs = work.tile([P, 2, P, 2], BF16, name="y_pairs", bufs=6)
+        pairs = work.tile([P, 2, P, 2], BF16, name="y_pairs", bufs=8)
         t["total", i, g] = total
         t["y_pairs", i, g] = pairs
         chunks = 4

@@ -36,7 +36,6 @@ def tile_lens_modes_pixel_intensity_g5_kernel(
         ident = keep.tile([P, P], F32, name="ident")
         gain_rows = keep.tile([P, 16], BF16, name="gain_rows")
         gain_all = keep.tile([P, PIXELS], BF16, name="gain_all")
-        table_warm = keep.tile([P, 1], F32, name="table_warm")
         y_scales = keep.tile([P, 4, FIELDS], U8, name="y_scales", align_bytes=64)
         y_codes = keep.tile([P, 4, FIELDS], U32, name="y_codes", align_bytes=64)
         t = {}
@@ -211,23 +210,6 @@ def tile_lens_modes_pixel_intensity_g5_kernel(
                 dst = t["w_plane", first][32 * q : 32 * q + 4, :, :].bitcast(I32)
                 nc.sync.dma_start(out=dst, in_=src.rearrange("k r n -> r k n"))
 
-        warm_in = keep.tile([P, 4 * P], BF16, name="warm_in", align_bytes=64)
-        warm_codes = keep.tile([P, P], U32, name="warm_codes", align_bytes=64)
-        warm_scales = keep.tile([P, P], U8, name="warm_scales", align_bytes=64)
-
-        def warm(count):
-            warm_acc = acc_pool.tile([P, P], F32, name=free_banks[0])
-            for n in range(count):
-                nc.tensor.matmul_mx(
-                    out=warm_acc[:],
-                    lhsT=warm_codes[:].bitcast(FP8X4),
-                    lhsT_scale=warm_scales[:],
-                    rhs=warm_codes[:].bitcast(FP8X4),
-                    rhs_scale=warm_scales[:],
-                    start=True,
-                    stop=True,
-                )
-
         def spread_gain():
             gain_words = gain_rows[:].bitcast(F32)
             all_words = gain_all[:].bitcast(F32).rearrange("p (n c) -> p n c", c=8)
@@ -303,12 +285,9 @@ def tile_lens_modes_pixel_intensity_g5_kernel(
             finish(i, g)
 
         nc.gpsimd.dma_start(out=gain_rows[:], in_=gain.rearrange("(p c) -> p c", p=P))
-        nc.vector.memset(warm_in[:], 1.0)
         clear_w_scales(*SCALE_LOADS[0])
-        nc.vector.quantize_mx(out=warm_codes[:].bitcast(FP8X4), scales=warm_scales[:], in_=warm_in[:])
         for first, count in SCALE_LOADS[1:]:
             clear_w_scales(first, count)
-        nc.scalar.activation(out=table_warm[:], in_=warm_in[:, 0:1], func=SQUARE)
         make_identity(nc, ident[:])
         load_fields(0, RE)
         load_w(0)
@@ -329,9 +308,7 @@ def tile_lens_modes_pixel_intensity_g5_kernel(
         load_fields(3, RE)
         load_fields(3, IM)
 
-        warm(19)
         fields(0, RE)
-        warm(5)
         spread_gain()
         multiply(0, RE, 0, weak)
         fields(0, IM)

from contextlib import ExitStack

import concourse.mybir as mybir
from concourse.masks import make_identity

F32 = mybir.dt.float32
BF16 = mybir.dt.bfloat16
I32 = mybir.dt.int32
U32 = mybir.dt.uint32
U8 = mybir.dt.uint8
FP8X4 = mybir.dt.float8_e4m3fn_x4
FP4X4 = mybir.dt.float4_e2m1fn_x4
ALU = mybir.AluOpType
SQUARE = mybir.ActivationFunctionType.Square

FIELDS, PIXELS, K_WEAK, K_CORE = 512, 2048, 1536, 512
FLOPS = 2 * (2 * FIELDS) * PIXELS * (K_WEAK + K_CORE)

P = 128
G = 512
WEAK_PASSES = 3
RE, IM = 0, 1
SCALE_LOADS = ((0, 2), (2, 2))


def tile_lens_modes_pixel_intensity_g5_kernel(
    tc, weak_field, weak_words, weak_scales, core_field, core_t, gain, out_0, out_1, out_2
):
    nc = tc.nc
    with ExitStack() as ctx:
        keep = ctx.enter_context(tc.tile_pool(name="keep", bufs=1))
        work = ctx.enter_context(tc.tile_pool(name="work", bufs=4))
        acc_pool = ctx.enter_context(tc.psum_pool(name="acc", bufs=1))
        ctx.enter_context(tc.manual_schedule())

        ident = keep.tile([P, P], F32, name="ident")
        gain_rows = keep.tile([P, 16], BF16, name="gain_rows")
        gain_all = keep.tile([P, PIXELS], BF16, name="gain_all")
        y_scales = keep.tile([P, 4, FIELDS], U8, name="y_scales", align_bytes=64)
        y_codes = keep.tile([P, 4, FIELDS], U32, name="y_codes", align_bytes=64)
        t = {}
        free_banks = ["acc_%d" % n for n in range(8)]

        def load_fields(i, part):
            rows = slice(part * FIELDS + i * P, part * FIELDS + (i + 1) * P)
            raw = keep.tile([P, K_WEAK + K_CORE], BF16, name="a_raw_%d_%d" % (i, part))
            nc.sync.dma_start(out=raw[:, :K_WEAK], in_=weak_field[rows, :])
            nc.sync.dma_start(out=raw[:, K_WEAK:], in_=core_field[rows, :])
            t["a_raw", i, part] = raw

        def load_w(g):
            words = keep.tile([P, WEAK_PASSES, 2 * G], U8, name="w_words_%d" % g, align_bytes=64)
            src = weak_words[:, :, 2 * G * g : 2 * G * (g + 1)].bitcast(I32)
            nc.sync.dma_start(out=words[:].bitcast(I32), in_=src.rearrange("k p n -> p k n"))
            t["w", g] = words

        def load_d(g):
            raw = keep.tile([P, 4, G], BF16, name="d_raw_%d" % g)
            nc.sync.dma_start(out=raw[:], in_=core_t[:, G * g : G * (g + 1)].rearrange("(p j) n -> p j n", j=4))
            t["d_raw", g] = raw

        def group_d(g):
            grouped = work.tile([P, G, 4], BF16, name="d_grouped", bufs=2, align_bytes=64)
            nc.vector.tensor_copy(
                out=grouped[:].rearrange("p (c i) j -> p c j i", i=4),
                in_=t["d_raw", g][:].rearrange("p j (c i) -> p c j i", i=4),
            )
            t["d_grouped", g] = grouped

        def quantize_d(g):
            codes = keep.tile([P, G], U32, name="d_codes_%d" % g, align_bytes=64)
            scales = keep.tile([P, G], U8, name="d_scales_%d" % g, align_bytes=64)
            nc.vector.quantize_mx(
                out=codes[:].bitcast(FP8X4), scales=scales[:], in_=t["d_grouped", g][:].rearrange("p n j -> p (n j)")
            )
            t["d", g] = (codes, scales)

        def split_words(i, part):
            split = work.tile([P, 4, 2, P], F32, name="a_split", bufs=2)
            words = t["a_raw", i, part][:].bitcast(F32)
            nc.scalar.copy(out=split[:], in_=words.rearrange("f (k p u) -> f k u p", k=4, u=2))
            t["a_split", i, part] = split

        def store_y_scales(half):
            cols = slice(2 * P * half, 2 * P * (half + 1))
            for q in range(4):
                dst = out_2[:, 4 * q : 4 * q + 4, cols].bitcast(I32).rearrange("g r m -> r g m")
                queue = nc.scalar if half and q % 2 else nc.sync
                queue.dma_start(out=dst, in_=y_scales[32 * q : 32 * q + 4, :, cols].bitcast(I32))

        def turn_fields(i, part, h):
            t["a_bank_name", i, part, h] = free_banks.pop(0)
            bank = acc_pool.tile([P, 2, 2, P], F32, name=t["a_bank_name", i, part, h])
            words = t["a_raw", i, part][:].bitcast(F32)
            for k in range(2):
                for u in range(2):
                    first = 256 * (2 * h + k)
                    if ("a_split", i, part) in t:
                        source = t["a_split", i, part][:, 2 * h + k, u, :]
                    else:
                        source = words[:, first + u : first + 256 : 2]
                    nc.tensor.transpose(bank[:, k, u, :], source, ident[:])
            t["a_bank", i, part, h] = bank

        def group_fields(i, part, h):
            grouped = work.tile([P, 2, P, 4], BF16, name="a_grouped", bufs=5, align_bytes=64)
            nc.scalar.copy(
                out=grouped[:].bitcast(F32), in_=t["a_bank", i, part, h][:].rearrange("p k u f -> p k f u")
            )
            t["a_grouped", i, part, h] = grouped
            free_banks.append(t["a_bank_name", i, part, h])

        def quantize_fields(i, part, h):
            codes = keep.tile([P, 2 * P], U32, name="a_codes_%d_%d_%d" % (i, part, h), align_bytes=64)
            scales = keep.tile([P, 2 * P], U8, name="a_scales_%d_%d_%d" % (i, part, h), align_bytes=64)
            nc.vector.quantize_mx(
                out=codes[:].bitcast(FP8X4),
                scales=scales[:],
                in_=t["a_grouped", i, part, h][:].rearrange("p k f t -> p (k f t)"),
            )
            t["a", i, part, h] = (codes, scales)

        def multiply(i, part, g, passes, first=0, width=G):
            pixels = slice(first, first + width)
            for k in passes:
                if k == 0:
                    t["bank", i, part, g] = free_banks.pop(0)
                    t["acc", i, part, g] = acc_pool.tile([P, width], F32, name=t["bank", i, part, g])
                codes, scales = t["a", i, part, k // 2]
                cols = slice(P * (k % 2), P * (k % 2 + 1))
                if k < WEAK_PASSES:
                    rhs = t["w", g][:, k, 2 * first : 2 * (first + width)].bitcast(FP4X4)
                    rhs_scale = t["w_scales", g][:, k, pixels]
                else:
                    rhs = t["d", g][0][:, pixels].bitcast(FP8X4)
                    rhs_scale = t["d", g][1][:, pixels]
                nc.tensor.matmul_mx(
                    out=t["acc", i, part, g][:],
                    lhsT=codes[:, cols].bitcast(FP8X4),
                    lhsT_scale=scales[:, cols],
                    rhs=rhs,
                    rhs_scale=rhs_scale,
                    start=(k == 0),
                    stop=(k == WEAK_PASSES),
                )

        def square(i, part, g):
            sq = work.tile([P, G], F32, name="sq", bufs=6)
            nc.scalar.activation(out=sq[:], in_=t["acc", i, part, g][:], func=SQUARE)
            t["sq", i, part, g] = sq
            free_banks.append(t["bank", i, part, g])

        def add_squares(i, g):
            total = work.tile([P, G], F32, name="total", bufs=3)
            nc.vector.tensor_tensor(out=total[:], in0=t["sq", i, RE, g][:], in1=t["sq", i, IM, g][:], op=ALU.add)
            t["total", i, g] = total

        def apply_gain(i, g):
            y = work.tile([P, G], F32, name="y", bufs=6)
            nc.vector.tensor_tensor(
                out=y[:], in0=t["total", i, g][:], in1=gain_all[:, G * g : G * (g + 1)], op=ALU.mult
            )
            nc.sync.dma_start(out=out_0[P * i : P * (i + 1), G * g : G * (g + 1)], in_=y[:])
            t["y", i, g] = y

        def round_y(i, g):
            pairs = work.tile([P, 2, P, 2], BF16, name="y_pairs", bufs=8)
            nc.vector.tensor_copy(out=pairs[:], in_=t["y", i, g][:].rearrange("f (p u e) -> f u p e", u=2, e=2))
            t["y_pairs", i, g] = pairs

        def turn_y(tiles, g):
            t["y_bank_name", tiles, g] = free_banks.pop(0)
            bank = acc_pool.tile([P, len(tiles), 2, P], F32, name=t["y_bank_name", tiles, g])
            for n, i in enumerate(tiles):
                words = t["y_pairs", i, g][:].rearrange("f u p e -> f u (p e)").bitcast(F32)
                for u in range(2):
                    nc.tensor.transpose(bank[:, n, u, :], words[:, u, :], ident[:])
            t["y_bank", tiles, g] = bank

        def group_y(tiles, g):
            grouped = work.tile([P, len(tiles), P, 4], BF16, name="y_grouped", bufs=5, align_bytes=64)
            nc.scalar.copy(
                out=grouped[:].bitcast(F32), in_=t["y_bank", tiles, g][:].rearrange("p n u f -> p n f u")
            )
            t["y_grouped", tiles, g] = grouped
            free_banks.append(t["y_bank_name", tiles, g])

        def quantize_y(tiles, g):
            cols = slice(P * tiles[0], P * (tiles[-1] + 1))
            nc.vector.quantize_mx(
                out=y_codes[:, g, cols].bitcast(FP8X4),
                scales=y_scales[:, g, cols],
                in_=t["y_grouped", tiles, g][:].rearrange("p n f t -> p (n f t)"),
            )
            if tiles[-1] % 2:
                half = slice(P * (tiles[-1] - 1), P * (tiles[-1] + 1))
                dst = out_1[g, :, half, :].rearrange("p m t -> p (m t)").bitcast(I32)
                nc.sync.dma_start(out=dst, in_=y_codes[:, g, half].bitcast(I32))

        def clear_w_scales(first, count):
            plane = keep.tile([P, WEAK_PASSES, count * G], U8, name="w_scales_%d" % first, align_bytes=64)
            nc.vector.memset(plane[:].bitcast(I32), 0)
            t["w_plane", first] = plane
            for n in range(count):
                t["w_scales", first + n] = plane[:, :, G * n : G * (n + 1)]

        def load_w_scales(first, count):
            for q in range(4):
                src = weak_scales[:, 4 * q : 4 * q + 4, G * first : G * (first + count)].bitcast(I32)
                dst = t["w_plane", first][32 * q : 32 * q + 4, :, :].bitcast(I32)
                nc.sync.dma_start(out=dst, in_=src.rearrange("k r n -> r k n"))

        def spread_gain():
            gain_words = gain_rows[:].bitcast(F32)
            all_words = gain_all[:].bitcast(F32).rearrange("p (n c) -> p n c", c=8)
            for b in range(2):
                bank_name = free_banks.pop(0)
                bank = acc_pool.tile([P, 4, P], F32, name=bank_name)
                for c in range(4):
                    column = gain_words[:, 4 * b + c : 4 * b + c + 1]
                    nc.tensor.transpose(bank[:, c, :], column.to_broadcast([P, P]), ident[:])
                nc.vector.tensor_copy(out=all_words[:, :, 4 * b : 4 * b + 4], in_=bank[:].rearrange("p c n -> p n c"))
                free_banks.append(bank_name)

        def prepare_fields(i, part):
            for h in range(2):
                turn_fields(i, part, h)
            for h in range(2):
                group_fields(i, part, h)

        def turn_pair(i, *units):
            for part in (RE, IM):
                for h in range(2):
                    turn_fields(i, part, h)
            for unit in units:
                turn_y(*unit)
            for part in (RE, IM):
                for h in range(2):
                    group_fields(i, part, h)
            for unit in units:
                group_y(*unit)

        def quantize_both(i, part):
            for h in range(2):
                quantize_fields(i, part, h)

        weak = range(WEAK_PASSES)
        core = [WEAK_PASSES]
        every = range(WEAK_PASSES + 1)

        def product(i, part, g, passes):
            multiply(i, part, g, passes)
            square(i, part, g)

        def products(i, g):
            for part in (RE, IM):
                product(i, part, g, every)

        def finish(i, g):
            add_squares(i, g)
            apply_gain(i, g)
            round_y(i, g)

        def fields(i, part):
            prepare_fields(i, part)
            quantize_both(i, part)

        def turn_planes(*units):
            for unit in units:
                turn_y(*unit)
            for unit in units:
                group_y(*unit)

        def planes(*units):
            turn_planes(*units)
            for unit in units:
                quantize_y(*unit)

        def core_operand(g):
            group_d(g)
            quantize_d(g)

        def tile(i, g):
            products(i, g)
            finish(i, g)

        nc.gpsimd.dma_start(out=gain_rows[:], in_=gain.rearrange("(p c) -> p c", p=P))
        clear_w_scales(*SCALE_LOADS[0])
        for first, count in SCALE_LOADS[1:]:
            clear_w_scales(first, count)
        make_identity(nc, ident[:])
        load_fields(0, RE)
        load_w(0)
        load_w_scales(0, 2)
        load_fields(0, IM)
        load_w(1)
        load_fields(1, RE)
        load_d(0)
        load_fields(1, IM)
        load_d(1)
        load_d(2)
        load_w_scales(2, 2)
        load_w(2)
        load_fields(2, RE)
        load_fields(2, IM)
        load_d(3)
        load_w(3)
        load_fields(3, RE)
        load_fields(3, IM)

        fields(0, RE)
        spread_gain()
        multiply(0, RE, 0, weak)
        fields(0, IM)
        multiply(0, RE, 1, weak)
        prepare_fields(1, RE)
        group_d(0)
        quantize_both(1, RE)
        quantize_d(0)
        multiply(0, IM, 0, weak)
        multiply(0, IM, 1, weak)
        group_d(1)
        prepare_fields(1, IM)
        quantize_fields(1, IM, 0)
        quantize_fields(1, IM, 1)
        quantize_d(1)
        multiply(1, RE, 0, weak)
        product(0, RE, 0, core)
        product(0, IM, 0, core)
        product(1, RE, 0, core)
        group_d(2)
        product(1, IM, 0, every)
        add_squares(0, 0)
        quantize_d(2)
        product(0, RE, 1, core)
        product(0, IM, 1, core)
        apply_gain(0, 0)
        add_squares(1, 0)
        round_y(0, 0)
        apply_gain(1, 0)
        add_squares(0, 1)
        round_y(1, 0)
        apply_gain(0, 1)
        product(1, RE, 1, every)
        split_words(2, RE)
        product(1, IM, 1, every)
        group_d(3)
        add_squares(1, 1)
        quantize_d(3)
        round_y(0, 1)
        apply_gain(1, 1)
        product(0, RE, 2, every)
        split_words(2, IM)
        product(0, IM, 2, every)
        add_squares(0, 2)
        round_y(1, 1)
        apply_gain(0, 2)
        product(1, RE, 2, every)
        product(1, IM, 2, every)
        add_squares(1, 2)
        round_y(0, 2)
        apply_gain(1, 2)
        turn_pair(2, ((0, 1), 0))
        quantize_both(2, RE)
        quantize_both(2, IM)
        product(0, RE, 3, every)
        product(0, IM, 3, every)
        quantize_y((0, 1), 0)
        add_squares(0, 3)
        round_y(1, 2)
        apply_gain(0, 3)
        product(1, RE, 3, every)
        product(1, IM, 3, every)
        add_squares(1, 3)
        round_y(0, 3)
        apply_gain(1, 3)
        product(2, RE, 0, every)
        split_words(3, RE)
        product(2, IM, 0, every)
        add_squares(2, 0)
        round_y(1, 3)
        apply_gain(2, 0)
        product(2, RE, 1, every)
        split_words(3, IM)
        product(2, IM, 1, every)
        add_squares(2, 1)
        round_y(2, 0)
        apply_gain(2, 1)
        product(2, RE, 2, every)
        product(2, IM, 2, every)
        add_squares(2, 2)
        round_y(2, 1)
        apply_gain(2, 2)
        turn_pair(3, ((0, 1), 1))
        quantize_both(3, RE)
        quantize_both(3, IM)
        product(2, RE, 3, every)
        product(2, IM, 3, every)
        quantize_y((0, 1), 1)
        add_squares(2, 3)
        round_y(2, 2)
        apply_gain(2, 3)
        product(3, RE, 0, every)
        product(3, IM, 0, every)
        add_squares(3, 0)
        round_y(2, 3)
        apply_gain(3, 0)
        product(3, RE, 1, every)
        product(3, IM, 1, every)
        add_squares(3, 1)
        round_y(3, 0)
        apply_gain(3, 1)
        turn_planes(((0, 1), 2), ((0, 1), 3), ((2,), 2), ((2,), 3))
        round_y(3, 1)
        quantize_y((0, 1), 2)
        quantize_y((0, 1), 3)
        store_y_scales(0)
        quantize_y((2,), 2)
        quantize_y((2,), 3)
        products(3, 2)
        turn_planes(((2, 3), 0), ((2, 3), 1))
        add_squares(3, 2)
        quantize_y((2, 3), 0)
        apply_gain(3, 2)
        quantize_y((2, 3), 1)
        round_y(3, 2)

        i, g = 3, 3
        product(i, RE, g, every)
        total = work.tile([P, G], F32, name="total", bufs=3)
        pairs = work.tile([P, 2, P, 2], BF16, name="y_pairs", bufs=8)
        t["total", i, g] = total
        t["y_pairs", i, g] = pairs
        chunks = 4
        width = G // chunks

        def gain_chunk(c):
            words = slice(c * width // 4, (c + 1) * width // 4)
            pixels = slice(c * width, (c + 1) * width)
            nc.vector.tensor_tensor(
                out=pairs[:, :, words, :],
                in0=total[:, pixels].rearrange("f (p u e) -> f u p e", u=2, e=2),
                in1=gain_all[:, G * g : G * (g + 1)][:, pixels].rearrange("f (p u e) -> f u p e", u=2, e=2),
                op=ALU.mult,
            )

        for c in range(chunks):
            pixels = slice(c * width, (c + 1) * width)
            multiply(i, IM, g, every, c * width, width)
            sq = work.tile([P, width], F32, name="sq_chunk")
            nc.scalar.activation(out=sq[:], in_=t["acc", i, IM, g][:], func=SQUARE)
            free_banks.append(t["bank", i, IM, g])
            nc.vector.tensor_tensor(out=total[:, pixels], in0=t["sq", i, RE, g][:, pixels], in1=sq[:], op=ALU.add)
            if c > 0:
                gain_chunk(c - 1)
        gain_chunk(chunks - 1)
        turn_planes(((3,), 2))
        apply_gain(3, 3)
        turn_planes(((3,), 3))
        quantize_y((3,), 2)
        quantize_y((3,), 3)
        store_y_scales(1)
